import numpy as np
CORES = [56,61,80,85]
N = 4
GR, GC = 2, 2
L, KA, KB, F = 2, 1, 1, 128
def setup_inputs(rng):
    return {"a": rng.standard_normal((N, 128, KA * 128), dtype=np.float32), "b": rng.standard_normal((N, 128, KB * F), dtype=np.float32)}
def setup_inputs_big(rng):
    d = setup_inputs(rng)
    for k in ("a", "b"): d[k] = (d[k].astype(np.float32) * 1024.0).astype(d[k].dtype)
    return d
def setup_inputs_small(rng):
    d = setup_inputs(rng)
    for k in ("a", "b"): d[k] = (d[k].astype(np.float32) * (1 / 1024.0)).astype(d[k].dtype)
    return d
def setup_inputs_apart(rng):
    d = setup_inputs(rng)
    f = (10.0 ** rng.permutation(np.linspace(-1.5, 1.5, N))).astype(np.float32).reshape(N, 1, 1)
    for k in ("a", "b"): d[k] = (d[k].astype(np.float32) * f).astype(d[k].dtype)
    return d
def reference(a, b):
    A, B = a.astype(np.float64), b.astype(np.float64)
    y = np.zeros((N, 128, F))
    for i in range(GR):
        for j in range(GC):
            for k in range(L):
                At = A[i * GC + k // KA][:, 128 * (k % KA):128 * (k % KA) + 128]
                Bt = B[(k // KB) * GC + j][:, F * (k % KB):F * (k % KB) + F]
                y[i * GC + j] += At.T @ Bt
    return {"y": y.astype(np.float32 if a.dtype != np.float64 else np.float64)}

@@ -1,0 +1,97 @@
+GR, GC = 2, 2
+N_ON = 4
+N_OFF = 8
+
+SCRATCH = {
+    "aS": ("sbuf", [128, 128], "float32"),
+    "bS": ("sbuf", [128, 128], "float32"),
+    "aR": ("sbuf", [128, 128], "float32"),
+    "bR": ("sbuf", [128, 128], "float32"),
+    "yS": ("sbuf", [128, 128], "float32"),
+    "bD": ("dram", [128, 128], "float32"),
+    "hD": ("dram", [128, 128], "float32"),
+    "ps": ("psum", [128, 128], "float32"),
+}
+SEMAPHORES = ["ldd", "lda", "ldb", "hop", "arra", "arrb", "sent", "mm", "cp", "stored"]
+
+
+def _pick(mask, n):
+    bits = [e for e in range(mask.bit_length()) if (mask >> e) & 1]
+    m = 0
+    for e in bits[::len(bits) // n][:n]:
+        m |= 1 << e
+    return m
+
+
+def _plan(T, topo):
+    cores = list(T.cores)
+    plan, used = {}, set()
+    for r, src in enumerate(cores):
+        i, j = divmod(r, GC)
+        b_to = cores[(1 - i) * GC + j]
+        a_to = cores[i * GC + (1 - j)]
+        cand = [h for h in range(topo.CHIPS * topo.CORES_PER_CHIP)
+                if topo.chip(h) == topo.chip(src) and h not in cores and h not in used
+                and topo.may_write(src, h) and topo.may_write(h, b_to)]
+        near = [h for h in cand if topo.die(h) == topo.die(src)]
+        relay = (near or cand)[0]
+        used.add(relay)
+        plan[src] = (b_to, a_to, relay)
+    return plan
+
+
+def rank_program(g, core, T, topo):
+    S = T.sem
+    plan = _plan(T, topo)
+
+    for src, (b_to, a_to, relay) in plan.items():
+        if relay == core:
+            rid, pid, _ = topo.addr(b_to)
+            g.wait_ge(S.hop, N_ON)
+            g.remote_dma(out_ap=T.bR[:], in_ap=T.hD[:], remote_sem=S.arrb, local_sem=S.sent, pid=pid, routing_id=rid,
+                         dma_engine_mask=_pick(topo.mask(core, b_to), N_OFF))
+            g.wait_ge(S.sent, N_OFF)
+            return
+
+    rank = T.rank_of(core)
+    if rank is None:
+        return
+    i, j = divmod(rank, GC)
+    b_to, a_to, relay = plan[core]
+
+    g.sync.dma_start(T.bD[:], T.b[:]).then_inc(S.ldd, 16)
+    g.scalar.dma_start(T.aS[:], T.a[:]).then_inc(S.lda, 16)
+    g.scalar.dma_start(T.bS[:], T.b[:]).then_inc(S.ldb, 16)
+
+    rid, pid, _ = topo.addr(relay)
+    g.wait_ge(S.ldd, 16)
+    g.remote_dma(out_ap=T.hD[:], in_ap=T.bD[:], remote_sem=S.hop, local_sem=S.sent, pid=pid, routing_id=rid,
+                 dma_engine_mask=_pick(topo.mask(core, relay), N_ON))
+    rid, pid, _ = topo.addr(a_to)
+    g.wait_ge(S.lda, 16)
+    g.remote_dma(out_ap=T.aR[:], in_ap=T.aS[:], remote_sem=S.arra, local_sem=S.sent, pid=pid, routing_id=rid,
+                 dma_engine_mask=_pick(topo.mask(core, a_to), N_ON))
+
+    te = g.tensor
+    te.wait_ge(S.ldb, 16)
+    if i == j:
+        te.wait_ge(S.lda, 16)
+        first, last = T.aS, T.aR
+    else:
+        te.wait_ge(S.arra, N_ON)
+        first, last = T.aR, T.aS
+    te.matmul(T.ps[:], first[:], T.bS[:], True, False)
+    if i == j:
+        te.wait_ge(S.arra, N_ON)
+    else:
+        te.wait_ge(S.lda, 16)
+    te.wait_ge(S.arrb, N_OFF)
+    te.matmul(T.ps[:], last[:], T.bR[:], False, True).then_inc(S.mm, 1)
+
+    g.vector.wait_ge(S.mm, 1)
+    g.vector.tensor_copy(T.yS[:], T.ps[:]).then_inc(S.cp, 1)
+    g.sync.wait_ge(S.cp, 1)
+    g.sync.dma_start(T.y[:], T.yS[:]).then_inc(S.stored, 16)
+    g.sync.wait_ge(S.stored, 16)
+
+    g.wait_ge(S.sent, 2 * N_ON)

@@ -1,5 +1,8 @@
 GR, GC = 2, 2
+W = [64, 64]
+OFF = [0, W[0]]
 N_ON = 4
+N_A = 8
 N_OFF = 8
 
 SCRATCH = {
@@ -8,11 +11,15 @@ SCRATCH = {
     "aR": ("sbuf", [128, 128], "float32"),
     "bR": ("sbuf", [128, 128], "float32"),
     "yS": ("sbuf", [128, 128], "float32"),
-    "bD": ("dram", [128, 128], "float32"),
-    "hD": ("dram", [128, 128], "float32"),
-    "ps": ("psum", [128, 128], "float32"),
+    "bD0": ("dram", [128, W[0]], "float32"),
+    "bD1": ("dram", [128, W[1]], "float32"),
+    "hD0": ("dram", [128, W[0]], "float32"),
+    "hD1": ("dram", [128, W[1]], "float32"),
+    "ps0": ("psum", [128, 512], "float32"),
+    "ps1": ("psum", [128, 512], "float32"),
 }
-SEMAPHORES = ["ldd", "lda", "ldb", "hop", "arra", "arrb", "sent", "mm", "cp", "stored"]
+SEMAPHORES = ["ld0", "ld1", "lda", "ldb", "hop", "arra", "arrb0", "arrb1", "sent",
+              "mm0", "mm1", "cp0", "cp1", "st0", "st1"]
 
 
 def _pick(mask, n):
@@ -25,18 +32,15 @@ def _pick(mask, n):
 
 def _plan(T, topo):
     cores = list(T.cores)
-    plan, used = {}, set()
+    plan = {}
     for r, src in enumerate(cores):
         i, j = divmod(r, GC)
         b_to = cores[(1 - i) * GC + j]
         a_to = cores[i * GC + (1 - j)]
-        cand = [h for h in range(topo.CHIPS * topo.CORES_PER_CHIP)
-                if topo.chip(h) == topo.chip(src) and h not in cores and h not in used
+        near = [h for h in range(topo.CHIPS * topo.CORES_PER_CHIP)
+                if topo.chip(h) == topo.chip(src) and topo.die(h) == topo.die(src) and h not in cores
                 and topo.may_write(src, h) and topo.may_write(h, b_to)]
-        near = [h for h in cand if topo.die(h) == topo.die(src)]
-        relay = (near or cand)[0]
-        used.add(relay)
-        plan[src] = (b_to, a_to, relay)
+        plan[src] = (b_to, a_to, near[:2])
     return plan
 
 
@@ -44,54 +48,62 @@ def rank_program(g, core, T, topo):
     S = T.sem
     plan = _plan(T, topo)
 
-    for src, (b_to, a_to, relay) in plan.items():
-        if relay == core:
-            rid, pid, _ = topo.addr(b_to)
-            g.wait_ge(S.hop, N_ON)
-            g.remote_dma(out_ap=T.bR[:], in_ap=T.hD[:], remote_sem=S.arrb, local_sem=S.sent, pid=pid, routing_id=rid,
-                         dma_engine_mask=_pick(topo.mask(core, b_to), N_OFF))
-            g.wait_ge(S.sent, N_OFF)
-            return
+    for src, (b_to, a_to, relays) in plan.items():
+        for h, relay in enumerate(relays):
+            if relay == core:
+                rid, pid, _ = topo.addr(b_to)
+                g.wait_ge(S.hop, N_ON)
+                g.remote_dma(out_ap=T.bR[:, OFF[h]:OFF[h] + W[h]], in_ap=T["hD%d" % h][:], remote_sem=S["arrb%d" % h],
+                             local_sem=S.sent, pid=pid, routing_id=rid,
+                             dma_engine_mask=_pick(topo.mask(core, b_to), N_OFF))
+                g.wait_ge(S.sent, N_OFF)
+                return
 
     rank = T.rank_of(core)
     if rank is None:
         return
     i, j = divmod(rank, GC)
-    b_to, a_to, relay = plan[core]
+    b_to, a_to, relays = plan[core]
 
-    g.sync.dma_start(T.bD[:], T.b[:]).then_inc(S.ldd, 16)
-    g.scalar.dma_start(T.aS[:], T.a[:]).then_inc(S.lda, 16)
-    g.scalar.dma_start(T.bS[:], T.b[:]).then_inc(S.ldb, 16)
+    for h in range(2):
+        g.sync.dma_start(T["bD%d" % h][:], T.b[:, OFF[h]:OFF[h] + W[h]]).then_inc(S["ld%d" % h], 16)
+    g.sync.dma_start(T.aS[:], T.a[:]).then_inc(S.lda, 16)
+    g.sync.dma_start(T.bS[:], T.b[:]).then_inc(S.ldb, 16)
 
-    rid, pid, _ = topo.addr(relay)
-    g.wait_ge(S.ldd, 16)
-    g.remote_dma(out_ap=T.hD[:], in_ap=T.bD[:], remote_sem=S.hop, local_sem=S.sent, pid=pid, routing_id=rid,
-                 dma_engine_mask=_pick(topo.mask(core, relay), N_ON))
+    for h in range(2):
+        rid, pid, _ = topo.addr(relays[h])
+        g.wait_ge(S["ld%d" % h], 16)
+        g.remote_dma(out_ap=T["hD%d" % h][:], in_ap=T["bD%d" % h][:], remote_sem=S.hop, local_sem=S.sent, pid=pid,
+                     routing_id=rid, dma_engine_mask=_pick(topo.mask(core, relays[h]), N_ON))
     rid, pid, _ = topo.addr(a_to)
     g.wait_ge(S.lda, 16)
     g.remote_dma(out_ap=T.aR[:], in_ap=T.aS[:], remote_sem=S.arra, local_sem=S.sent, pid=pid, routing_id=rid,
-                 dma_engine_mask=_pick(topo.mask(core, a_to), N_ON))
+                 dma_engine_mask=_pick(topo.mask(core, a_to), N_A))
 
     te = g.tensor
+    ps = [T.ps0, T.ps1]
     te.wait_ge(S.ldb, 16)
     if i == j:
         te.wait_ge(S.lda, 16)
         first, last = T.aS, T.aR
     else:
-        te.wait_ge(S.arra, N_ON)
+        te.wait_ge(S.arra, N_A)
         first, last = T.aR, T.aS
-    te.matmul(T.ps[:], first[:], T.bS[:], True, False)
+    for h in range(2):
+        te.matmul(ps[h][:, 0:W[h]], first[:], T.bS[:, OFF[h]:OFF[h] + W[h]], True, False)
     if i == j:
-        te.wait_ge(S.arra, N_ON)
+        te.wait_ge(S.arra, N_A)
     else:
         te.wait_ge(S.lda, 16)
-    te.wait_ge(S.arrb, N_OFF)
-    te.matmul(T.ps[:], last[:], T.bR[:], False, True).then_inc(S.mm, 1)
+    for h in range(2):
+        te.wait_ge(S["arrb%d" % h], N_OFF)
+        te.matmul(ps[h][:, 0:W[h]], last[:], T.bR[:, OFF[h]:OFF[h] + W[h]], False, True).then_inc(S["mm%d" % h], 1)
 
-    g.vector.wait_ge(S.mm, 1)
-    g.vector.tensor_copy(T.yS[:], T.ps[:]).then_inc(S.cp, 1)
-    g.sync.wait_ge(S.cp, 1)
-    g.sync.dma_start(T.y[:], T.yS[:]).then_inc(S.stored, 16)
-    g.sync.wait_ge(S.stored, 16)
+    for h, q in enumerate((g.scalar, g.sync)):
+        g.vector.wait_ge(S["mm%d" % h], 1)
+        g.vector.tensor_copy(T.yS[:, OFF[h]:OFF[h] + W[h]], ps[h][:, 0:W[h]]).then_inc(S["cp%d" % h], 1)
+        q.wait_ge(S["cp%d" % h], 1)
+        q.dma_start(T.y[:, OFF[h]:OFF[h] + W[h]], T.yS[:, OFF[h]:OFF[h] + W[h]]).then_inc(S["st%d" % h], 16)
+        q.wait_ge(S["st%d" % h], 16)
 
-    g.wait_ge(S.sent, 2 * N_ON)
+    g.wait_ge(S.sent, 2 * N_ON + N_A)

GR, GC = 2, 2
W = [64, 64]
OFF = [0, W[0]]
N_ON = 4
N_A = 8
N_OFF = 8

SCRATCH = {
    "aS": ("sbuf", [128, 128], "float32"),
    "bS": ("sbuf", [128, 128], "float32"),
    "aR": ("sbuf", [128, 128], "float32"),
    "bR": ("sbuf", [128, 128], "float32"),
    "yS": ("sbuf", [128, 128], "float32"),
    "bD0": ("dram", [128, W[0]], "float32"),
    "bD1": ("dram", [128, W[1]], "float32"),
    "hD0": ("dram", [128, W[0]], "float32"),
    "hD1": ("dram", [128, W[1]], "float32"),
    "ps0": ("psum", [128, 512], "float32"),
    "ps1": ("psum", [128, 512], "float32"),
}
SEMAPHORES = ["ld0", "ld1", "lda", "ldb", "hop", "arra", "arrb0", "arrb1", "sent",
              "mm0", "mm1", "cp0", "cp1", "st0", "st1"]


def _pick(mask, n):
    bits = [e for e in range(mask.bit_length()) if (mask >> e) & 1]
    m = 0
    for e in bits[::len(bits) // n][:n]:
        m |= 1 << e
    return m


def _plan(T, topo):
    cores = list(T.cores)
    plan = {}
    for r, src in enumerate(cores):
        i, j = divmod(r, GC)
        b_to = cores[(1 - i) * GC + j]
        a_to = cores[i * GC + (1 - j)]
        near = [h for h in range(topo.CHIPS * topo.CORES_PER_CHIP)
                if topo.chip(h) == topo.chip(src) and topo.die(h) == topo.die(src) and h not in cores
                and topo.may_write(src, h) and topo.may_write(h, b_to)]
        plan[src] = (b_to, a_to, near[:2])
    return plan


def rank_program(g, core, T, topo):
    S = T.sem
    plan = _plan(T, topo)

    for src, (b_to, a_to, relays) in plan.items():
        for h, relay in enumerate(relays):
            if relay == core:
                rid, pid, _ = topo.addr(b_to)
                g.wait_ge(S.hop, N_ON)
                g.remote_dma(out_ap=T.bR[:, OFF[h]:OFF[h] + W[h]], in_ap=T["hD%d" % h][:], remote_sem=S["arrb%d" % h],
                             local_sem=S.sent, pid=pid, routing_id=rid,
                             dma_engine_mask=_pick(topo.mask(core, b_to), N_OFF))
                g.wait_ge(S.sent, N_OFF)
                return

    rank = T.rank_of(core)
    if rank is None:
        return
    i, j = divmod(rank, GC)
    b_to, a_to, relays = plan[core]

    for h in range(2):
        g.sync.dma_start(T["bD%d" % h][:], T.b[:, OFF[h]:OFF[h] + W[h]]).then_inc(S["ld%d" % h], 16)
    g.sync.dma_start(T.aS[:], T.a[:]).then_inc(S.lda, 16)
    g.sync.dma_start(T.bS[:], T.b[:]).then_inc(S.ldb, 16)

    for h in range(2):
        rid, pid, _ = topo.addr(relays[h])
        g.wait_ge(S["ld%d" % h], 16)
        g.remote_dma(out_ap=T["hD%d" % h][:], in_ap=T["bD%d" % h][:], remote_sem=S.hop, local_sem=S.sent, pid=pid,
                     routing_id=rid, dma_engine_mask=_pick(topo.mask(core, relays[h]), N_ON))
    rid, pid, _ = topo.addr(a_to)
    g.wait_ge(S.lda, 16)
    g.remote_dma(out_ap=T.aR[:], in_ap=T.aS[:], remote_sem=S.arra, local_sem=S.sent, pid=pid, routing_id=rid,
                 dma_engine_mask=_pick(topo.mask(core, a_to), N_A))

    te = g.tensor
    ps = [T.ps0, T.ps1]
    te.wait_ge(S.ldb, 16)
    if i == j:
        te.wait_ge(S.lda, 16)
        first, last = T.aS, T.aR
    else:
        te.wait_ge(S.arra, N_A)
        first, last = T.aR, T.aS
    for h in range(2):
        te.matmul(ps[h][:, 0:W[h]], first[:], T.bS[:, OFF[h]:OFF[h] + W[h]], True, False)
    if i == j:
        te.wait_ge(S.arra, N_A)
    else:
        te.wait_ge(S.lda, 16)
    for h in range(2):
        te.wait_ge(S["arrb%d" % h], N_OFF)
        te.matmul(ps[h][:, 0:W[h]], last[:], T.bR[:, OFF[h]:OFF[h] + W[h]], False, True).then_inc(S["mm%d" % h], 1)

    for h, q in enumerate((g.scalar, g.sync)):
        g.vector.wait_ge(S["mm%d" % h], 1)
        g.vector.tensor_copy(T.yS[:, OFF[h]:OFF[h] + W[h]], ps[h][:, 0:W[h]]).then_inc(S["cp%d" % h], 1)
        q.wait_ge(S["cp%d" % h], 1)
        q.dma_start(T.y[:, OFF[h]:OFF[h] + W[h]], T.yS[:, OFF[h]:OFF[h] + W[h]]).then_inc(S["st%d" % h], 16)
        q.wait_ge(S["st%d" % h], 16)

    g.wait_ge(S.sent, 2 * N_ON + N_A)
